import numpy as np
import ml_dtypes


def mxq(x, axis, fmt="e4m3"):
    dtype, down = {"e4m3": (ml_dtypes.float8_e4m3fn, 7), "e5m2": (ml_dtypes.float8_e5m2, 14)}[fmt]
    v = np.moveaxis(np.asarray(x, np.float32).astype(ml_dtypes.bfloat16).astype(np.float64), axis, -1)
    blocks = v.reshape(v.shape[:-1] + (-1, 32))
    amax = np.abs(blocks).max(-1, keepdims=True)
    byte = np.maximum(np.where(amax > 0, np.frexp(amax)[1] - 1 + 127, 0) - down, 1)
    scale = np.exp2(byte - 127.0)
    codes = (blocks / scale).astype(np.float32).astype(dtype).astype(np.float64)
    return np.moveaxis((codes * scale).reshape(v.shape), -1, axis)


WIDE = False


def mx_kscale(k):
    if not WIDE:
        return np.ones(k)
    levels = np.array([10, -10, 5, -5, 0])
    if k % 512:
        return np.exp2(np.random.permutation(np.resize(levels, k // 32))).repeat(32)
    a = np.empty((k // 512, 16))
    for p in range(k // 512):
        a[p, :8] = np.random.permutation(np.resize(levels, 8))
        for g in range(8):
            far = levels[np.abs(levels - a[p, g]) >= 10]
            a[p, g + 8] = far[np.random.randint(len(far))]
    return np.exp2(a.ravel()).repeat(32)


def f64(x):
    return np.asarray(x).astype(np.float64)


def striped(idx):
    return np.tile(idx.reshape(-1, 16).T, (8, 1)).astype(np.uint16)


def unstriped(offs):
    return offs[:16].T.reshape(-1).astype(np.int64)


def striped8(idx):
    return np.concatenate([x.reshape(-1, 16).T for x in idx]).astype(np.uint16)


def runs(offs, k):
    lists = np.stack([offs[16 * r : 16 * r + 16].T.reshape(-1) for r in range(8)]).astype(np.int64)
    return lists[np.arange(k) % 512 // 64]


def pack_weight(w):
    k, n = w.shape
    w = f64(np.asarray(w, np.float32).astype(ml_dtypes.bfloat16)).reshape(k // 32, 32, n)
    amax = np.abs(w).max(1)
    byte = np.clip(np.where(amax > 0, np.frexp(amax)[1] - 1 + 127 - 7, 1), 1, 254)
    scaled = (w * np.exp2(127.0 - byte)[:, None, :]).reshape(k, n).astype(np.float32)
    words = np.ascontiguousarray(scaled.reshape(k // 512, 128, 4, n).transpose(0, 1, 3, 2)).astype(ml_dtypes.float8_e4m3fn).view(np.uint8)
    return words, np.ascontiguousarray(byte.astype(np.uint8).reshape(k // 512, 16, n))


def unpack_weight(words, scales):
    g, p, n, _ = words.shape
    vals = np.ascontiguousarray(words).view(ml_dtypes.float8_e4m3fn).astype(np.float64) * np.repeat(np.exp2(scales.astype(np.float64) - 127.0), 8, axis=1)[..., None]
    return vals.transpose(0, 1, 3, 2).reshape(g * 512, n)


E2M1 = np.array([0.0, 0.5, 1.0, 1.5, 2.0, 3.0, 4.0, 6.0, -0.0, -0.5, -1.0, -1.5, -2.0, -3.0, -4.0, -6.0])


def pack_fp4(w):
    k, n = w.shape
    w = f64(np.asarray(w, np.float32).astype(ml_dtypes.bfloat16)).reshape(k // 32, 32, n)
    amax = np.abs(w).max(1)
    mant, ex = np.frexp(amax / 6.0)
    byte = np.clip(np.where(amax > 0, np.where(mant > 0.5, ex, ex - 1) + 127, 1), 1, 254)
    scaled = (w * np.exp2(127.0 - byte)[:, None, :]).reshape(k, n).astype(np.float32)
    c = np.ascontiguousarray(scaled.reshape(k // 512, 128, 4, n).transpose(0, 1, 3, 2)).astype(ml_dtypes.float4_e2m1fn).view(np.uint8) & 0xF
    words = (c[..., 0::2] | (c[..., 1::2] << 4)).reshape(k // 512, 128, 2 * n)
    return np.ascontiguousarray(words), np.ascontiguousarray(byte.astype(np.uint8).reshape(k // 512, 16, n))


def unpack_fp4(words, scales):
    g, _, n = scales.shape
    words = np.ascontiguousarray(words).reshape(g, 128, n, 2)
    nib = np.empty((g, 128, n, 4), np.uint8)
    nib[..., 0::2] = words & 0xF
    nib[..., 1::2] = words >> 4
    vals = E2M1[nib] * np.repeat(np.exp2(scales.astype(np.float64) - 127.0), 8, axis=1)[..., None]
    return vals.transpose(0, 1, 3, 2).reshape(g * 512, n)


def sigmoid(v):
    return 1.0 / (1.0 + np.exp(-np.maximum(v, -700.0)))


K, T, S, N, G, H, W = 512, 1024, 512, 512, 2048, 512, 256


def setup_inputs():
    n = np.random.standard_normal
    s = mx_kscale(K)[:, None]
    u = mx_kscale(S)
    packed_xT = pack_weight(n((K, T)) * s)
    packed_dT = pack_weight(n((K, G)) / s)
    packed_w1 = pack_fp4(n((H, N)) / np.sqrt(2 * H) / u[:, None])
    packed_w2 = pack_fp4(n((K, N)) / np.sqrt(2 * K) / s)
    perm = np.random.permutation(S)
    perm2 = np.random.permutation(S)
    perm3 = np.stack([np.random.permutation(S) for _ in range(8)])
    perm4 = np.stack([np.random.permutation(S) for _ in range(8)])
    return {
        "x_words": packed_xT[0],
        "x_scales": packed_xT[1],
        "d_words": packed_dT[0],
        "d_scales": packed_dT[1],
        "gn": (np.random.uniform(0.5, 1.5, (H, 1)) * u[:, None]).astype(np.float32),
        "w1_words": packed_w1[0],
        "w1_scales": packed_w1[1],
        "w2_words": packed_w2[0],
        "w2_scales": packed_w2[1],
        "sl": np.random.uniform(1.0, 2.0, (N, 1)).astype(np.float32),
        "th": (0.5 * n((N, 1))).astype(np.float32),
        "offs": striped8(np.random.randint(0, T, (8, S))),
        "k1": striped8(np.random.randint(0, G, (8, H))),
        "hz": striped8(np.random.randint(0, T, (8, S))),
        "k2": striped8(np.random.randint(0, G, (8, H))),
        "n1": striped(perm[:W]),
        "n2": striped(perm[W:]),
        "n3": striped(perm2[:W]),
        "n4": striped(perm2[W:]),
        "n5": striped(np.random.permutation(S)),
        "two": striped(np.random.permutation(T)[:S]),
        "n6": striped8(perm3[:, :W]),
        "n7": striped8(perm3[:, W:]),
        "n8": striped8(perm4[:, :W]),
        "n9": striped8(perm4[:, W:]),
        "n10": striped8(np.stack([np.random.permutation(S) for _ in range(8)])),
    }


def reference(x_words, x_scales, d_words, d_scales, gn, w1_words, w1_scales, w2_words, w2_scales, sl, th, offs, k1, hz, k2, n1, n2, n3, n4, n5, two, n6, n7, n8, n9, n10):
    d_k1 = unpack_weight(d_words, d_scales)[np.arange(K)[:, None], runs(k1, K)]
    xq = unpack_weight(x_words, x_scales)[np.arange(K)[:, None], runs(offs, K)]
    d_k2 = unpack_weight(d_words, d_scales)[np.arange(K)[:, None], runs(k2, K)]
    x_hz = unpack_weight(x_words, x_scales)[np.arange(K)[:, None], runs(hz, K)]
    h = 0.0625 * (d_k1.T @ xq + d_k2.T @ x_hz)
    pa = h[:, unstriped(n1)]
    pb = h[:, unstriped(n2)]
    rb = np.maximum(pa, pb)
    ra = pa + pb
    ua = np.zeros((H, S))
    ua[:, unstriped(n3)] = ra
    ub = ua.copy()
    ub[:, unstriped(n4)] = rb
    z = f64(gn) * (ub - ub[:, unstriped(n5)])
    x_two = unpack_weight(x_words, x_scales)[:, unstriped(two)]
    h2 = unpack_fp4(w1_words, w1_scales).T @ mxq(z, 0, "e4m3") + unpack_fp4(w2_words, w2_scales).T @ x_two
    pa2 = h2[np.arange(N)[:, None], runs(n6, N)]
    pb2 = h2[np.arange(N)[:, None], runs(n7, N)]
    rb2 = np.minimum(pa2, pb2)
    ra2 = np.maximum(pa2, pb2)
    ua2 = np.zeros((N, S))
    ua2[np.arange(N)[:, None], runs(n8, N)] = ra2
    ub2 = ua2.copy()
    ub2[np.arange(N)[:, None], runs(n9, N)] = rb2
    sg = sigmoid(f64(sl) * (ub2[np.arange(N)[:, None], runs(n10, N)] - f64(th)))
    return ub2 * sg

@@ -1,0 +1,243 @@
+from contextlib import ExitStack
+
+import concourse.mybir as mybir
+
+F32 = mybir.dt.float32
+BF16 = mybir.dt.bfloat16
+I32 = mybir.dt.int32
+U32 = mybir.dt.uint32
+U16 = mybir.dt.uint16
+U8 = mybir.dt.uint8
+FP8X4 = mybir.dt.float8_e4m3fn_x4
+FP4X4 = mybir.dt.float4_e2m1fn_x4
+ALU = mybir.AluOpType
+ACT = mybir.ActivationFunctionType
+
+P = 128
+T, G, S, W = 1024, 2048, 512, 256
+FLOPS = 4 * 2 * 512 * 512 * 512
+
+
+def entries(lst, first, count):
+    return lst[:, first // 16 : (first + count) // 16]
+
+
+def tile_picked_mhhzntcphdeord_none_p_kernel(
+    tc, x_words, x_scales, d_words, d_scales, gn, w1_words, w1_scales, w2_words, w2_scales, sl, th,
+    offs, k1, hz, k2, n1, n2, n3, n4, n5, two, n6, n7, n8, n9, n10, out,
+):
+    nc = tc.nc
+    with ExitStack() as ctx:
+        lists = ctx.enter_context(tc.tile_pool(name="lists", bufs=1))
+        keep = ctx.enter_context(tc.tile_pool(name="keep", bufs=1))
+        shared = ctx.enter_context(tc.tile_pool(name="shared", bufs=1))
+        psum = ctx.enter_context(tc.psum_pool(name="psum", bufs=8))
+
+        def load_list(name, src):
+            tile = lists.tile([P, src.shape[1]], U16, name=name)
+            nc.sync.dma_start(tile[:], src)
+            return tile
+
+        def zeroed_bytes(name, width, engine):
+            tile = keep.tile([P, width], U8, name=name, align_bytes=64)
+            engine.memset(tile[:].bitcast(I32), 0)
+            return tile
+
+        def place_scale_rows(dst, src):
+            for q in range(4):
+                nc.sync.dma_start(dst[32 * q : 32 * q + 4, :].bitcast(I32), src[32 * q : 32 * q + 32 : 8, :].bitcast(I32))
+
+        ws_raw = zeroed_bytes("ws_raw", 2 * S, nc.gpsimd)
+        d_s = zeroed_bytes("d_s", 2 * S, nc.vector)
+        x_s = zeroed_bytes("x_s", 2 * S, nc.vector)
+        two_s = zeroed_bytes("two_s", S, nc.vector)
+
+        ds_win = keep.tile([P, G], U8, name="ds_win")
+        xs_win = keep.tile([P, T], U8, name="xs_win")
+        k1_t = load_list("k1_t", k1)
+        nc.scalar.dma_start(ds_win[:].bitcast(I32), d_scales[0].bitcast(I32).unsqueeze(1).to_broadcast([16, 8, G // 4]))
+        nc.scalar.dma_start(xs_win[:].bitcast(I32), x_scales[0].bitcast(I32).unsqueeze(1).to_broadcast([16, 8, T // 4]))
+        k2_t = load_list("k2_t", k2)
+        offs_t = load_list("offs_t", offs)
+        hz_t = load_list("hz_t", hz)
+        xw_win = keep.tile([P, T], U32, name="xw_win")
+        nc.sync.dma_start(xw_win[:].bitcast(I32), x_words[0].rearrange("p n r -> p (n r)").bitcast(I32))
+        dw_win = keep.tile([P, G], U32, name="dw_win")
+        nc.sync.dma_start(dw_win[:].bitcast(I32), d_words[0].rearrange("p n r -> p (n r)").bitcast(I32))
+        n1_t = load_list("n1_t", n1)
+        n2_t = load_list("n2_t", n2)
+        n3_t = load_list("n3_t", n3)
+        two_t = load_list("two_t", two)
+        n4_t = load_list("n4_t", n4)
+        n5_t = load_list("n5_t", n5)
+        w_raw = []
+        for a, words in enumerate((w1_words, w2_words)):
+            raw = keep.tile([P, 2 * S], U8, name="w_raw%d" % a)
+            nc.sync.dma_start(raw[:].bitcast(I32), words[0].bitcast(I32))
+            w_raw.append(raw)
+        n6_t = load_list("n6_t", n6)
+        n7_t = load_list("n7_t", n7)
+        n8_t = load_list("n8_t", n8)
+        n9_t = load_list("n9_t", n9)
+        n10_t = load_list("n10_t", n10)
+        for a, scales in enumerate((w1_scales, w2_scales)):
+            for q in range(4):
+                nc.gpsimd.dma_start(
+                    ws_raw[32 * q : 32 * q + 4, a * S : (a + 1) * S].bitcast(I32), scales[0, 4 * q : 4 * q + 4, :].bitcast(I32)
+                )
+        gn_t = keep.tile([P, 4], F32, name="gn_t")
+        sl_t = keep.tile([P, 4], F32, name="sl_t")
+        th_t = keep.tile([P, 4], F32, name="th_t")
+        for tile, src in ((gn_t, gn), (sl_t, sl), (th_t, th)):
+            nc.gpsimd.dma_start(tile[:], src.rearrange("(p t) o -> p (t o)", t=4))
+        neg_gn = keep.tile([P, 4], F32, name="neg_gn")
+        nc.gpsimd.tensor_scalar(neg_gn[:], gn_t[:], -1.0, 0.0, ALU.mult, ALU.add)
+        sl_th = keep.tile([P, 4], F32, name="sl_th")
+        nc.gpsimd.tensor_tensor(sl_th[:], sl_t[:], th_t[:], ALU.mult)
+        sg_bias = keep.tile([P, 4], F32, name="sg_bias")
+        nc.gpsimd.tensor_scalar(sg_bias[:], sl_th[:], -1.0, 0.0, ALU.mult, ALU.add)
+
+        ds_picked = keep.tile([P, 2, S], U8, name="ds_picked")
+        xs_picked = keep.tile([P, 2, S], U8, name="xs_picked")
+        ds_dealt = keep.tile([P, 2, 4, P], U8, name="ds_dealt")
+        for a, lst in enumerate((k1_t, k2_t)):
+            nc.vector.tensor_copy(ds_picked[:, a, :], ds_win[:].indirect(lst[:]))
+        nc.vector.tensor_copy(xs_picked[:, 0, :], xs_win[:].indirect(offs_t[:]))
+        nc.vector.tensor_copy(ds_dealt[:].rearrange("p a t m -> p a m t"), ds_picked[:].rearrange("p a (m t) -> p a m t", t=4))
+        place_scale_rows(d_s, ds_dealt[:].rearrange("p a t m -> p (a t m)"))
+        nc.vector.tensor_copy(xs_picked[:, 1, :], xs_win[:].indirect(hz_t[:]))
+        place_scale_rows(x_s, xs_picked[:].rearrange("p a c -> p (a c)"))
+
+        d_w, x_w = [], []
+        for a, (d_lst, x_lst) in enumerate(((k1_t, offs_t), (k2_t, hz_t))):
+            picked = shared.tile([P, S], U32, name="dw_picked%d" % a, offset=4096 * a, align_bytes=64)
+            nc.vector.tensor_copy(picked[:], dw_win[:].indirect(d_lst[:]))
+            xw = keep.tile([P, S], U32, name="x_w%d" % a, align_bytes=64)
+            nc.vector.tensor_copy(xw[:], xw_win[:].indirect(x_lst[:]))
+            x_w.append(xw)
+            dealt = keep.tile([P, 4, P], U32, name="d_w%d" % a, align_bytes=64)
+            nc.vector.tensor_copy(dealt[:].rearrange("p t m -> p m t"), picked[:].rearrange("p (m t) -> p m t", t=4))
+            d_w.append(dealt)
+
+        h_bank = [psum.tile([P, S], F32, name="h_bank%d" % t, tag="bank") for t in range(4)]
+        for a in range(2):
+            for t in range(4):
+                nc.tensor.matmul_mx(
+                    h_bank[t][:], lhsT=d_w[a][:, t, :].bitcast(FP8X4), lhsT_scale=d_s[:, a * S + t * P : a * S + (t + 1) * P],
+                    rhs=x_w[a][:].bitcast(FP8X4), rhs_scale=x_s[:, a * S : (a + 1) * S],
+                    start=(a == 0), stop=(a == 1),
+                )
+
+        two_picked = shared.tile([P, S], U8, name="two_picked", offset=4096 - 448, align_bytes=64)
+        w_s = shared.tile([P, 2, 4, P], U8, name="w_s", offset=4096 + 64, align_bytes=64)
+        two_w = shared.tile([P, S], U32, name="two_w", offset=4096 + 64 + 1024, align_bytes=64)
+        nc.vector.tensor_copy(two_picked[:], xs_win[:].indirect(two_t[:]))
+        place_scale_rows(two_s, two_picked)
+        nc.vector.tensor_copy(two_w[:], xw_win[:].indirect(two_t[:]))
+        nc.vector.tensor_copy(w_s[:].rearrange("p a t m -> p a m t"), ws_raw[:].rearrange("p (a m t) -> p a m t", a=2, t=4))
+        w_w = []
+        for a in range(2):
+            dealt = keep.tile([P, 4, 2 * P], U8, name="w_w%d" % a, align_bytes=64)
+            nc.scalar.copy(dealt[:].bitcast(U16), w_raw[a][:].bitcast(U16).rearrange("p (m t) -> p t m", t=4))
+            w_w.append(dealt)
+
+        z_planes = keep.tile([P, 4, S], BF16, name="z_planes")
+        ub = []
+
+        def finish_z(t):
+            scaled = keep.tile([P, S], F32, name="scaled%d" % t)
+            far = keep.tile([P, S], F32, name="far%d" % t)
+            nc.scalar.activation(scaled[:], ub[t][:], ACT.Copy, scale=gn_t[:, t : t + 1])
+            for first in (0, W):
+                nc.scalar.activation(far[:, first : first + W], scaled[:].indirect(entries(n5_t, first, W)), ACT.Copy)
+            nc.vector.tensor_tensor(z_planes[:, t, :], scaled[:], far[:], ALU.subtract)
+
+        for t in range(4):
+            h = keep.tile([P, S], F32, name="h%d" % t)
+            nc.scalar.activation(h[:], h_bank[t][:], ACT.Copy, scale=0.0625)
+            pa = keep.tile([P, W], F32, name="pa%d" % t)
+            pb = keep.tile([P, W], F32, name="pb%d" % t)
+            rb = keep.tile([P, W], F32, name="rb%d" % t)
+            u = keep.tile([P, S], F32, name="ub%d" % t)
+            ub.append(u)
+            piece = W // 2 if t == 0 else W
+            for first in range(0, W, piece):
+                cols = slice(first, first + piece)
+                nc.scalar.activation(pa[:, cols], h[:].indirect(entries(n1_t, first, piece)), ACT.Copy)
+                nc.scalar.activation(pb[:, cols], h[:].indirect(entries(n2_t, first, piece)), ACT.Copy)
+                nc.vector.tensor_tensor(u[:].indirect(entries(n3_t, first, piece)), pa[:, cols], pb[:, cols], ALU.add)
+                nc.vector.tensor_tensor(rb[:, cols], pa[:, cols], pb[:, cols], ALU.max)
+            if t > 0:
+                finish_z(t - 1)
+            nc.vector.tensor_copy(u[:].indirect(n4_t[:]), rb[:])
+
+        scaled = keep.tile([P, S], F32, name="scaled3")
+        far = keep.tile([P, S], F32, name="far3")
+        nc.vector.tensor_scalar(scaled[:], ub[3][:], gn_t[:, 3:4], None, ALU.mult)
+        for first in (0, W):
+            cols = slice(first, first + W)
+            nc.scalar.activation(far[:, cols], ub[3][:].indirect(entries(n5_t, first, W)), ACT.Copy)
+            nc.vector.scalar_tensor_tensor(z_planes[:, 3, cols], far[:, cols], neg_gn[:, 3:4], scaled[:, cols], ALU.mult, ALU.add)
+        grouped = [keep.tile([P, W, 4], BF16, name="grouped%d" % half, align_bytes=64) for half in range(2)]
+        nc.scalar.copy(grouped[0][:], z_planes[:, :, 0:W].rearrange("p t c -> p c t"))
+        nc.vector.tensor_copy(grouped[1][:], z_planes[:, :, W:S].rearrange("p t c -> p c t"))
+        z_w = [keep.tile([P, W], U32, name="z_w%d" % half, align_bytes=64) for half in range(2)]
+        z_s = [keep.tile([P, W], U8, name="z_s%d" % half, align_bytes=64) for half in range(2)]
+        for half in (1, 0):
+            nc.vector.quantize_mx(z_w[half][:].bitcast(FP8X4), z_s[half][:], grouped[half][:].rearrange("p c t -> p (c t)"))
+
+        h2_bank = [[psum.tile([P, W], F32, name="h2_bank%d_%d" % (t, half), tag="bank") for half in range(2)] for t in range(4)]
+        for t in range(4):
+            for half in range(2):
+                nc.tensor.matmul_mx(
+                    h2_bank[t][half][:], lhsT=w_w[1][:, t, :].bitcast(FP4X4), lhsT_scale=w_s[:, 1, t, :],
+                    rhs=two_w[:, half * W : (half + 1) * W].bitcast(FP8X4), rhs_scale=two_s[:, half * W : (half + 1) * W],
+                    start=True, stop=False,
+                )
+        for t in range(4):
+            for half in (1, 0):
+                nc.tensor.matmul_mx(
+                    h2_bank[t][half][:], lhsT=w_w[0][:, t, :].bitcast(FP4X4), lhsT_scale=w_s[:, 0, t, :],
+                    rhs=z_w[half][:].bitcast(FP8X4), rhs_scale=z_s[half][:],
+                    start=False, stop=True,
+                )
+
+        out_rows = out.rearrange("(p t) j -> t p j", t=4)
+        ub2 = []
+
+        def finish_out(t):
+            sg = keep.tile([P, S], F32, name="sg%d" % t)
+            res = keep.tile([P, S], F32, name="res%d" % t)
+            for first in (0, W):
+                nc.scalar.activation(
+                    sg[:, first : first + W], ub2[t][:].indirect(entries(n10_t, first, W)), ACT.Sigmoid,
+                    scale=sl_t[:, t : t + 1], bias=sg_bias[:, t : t + 1],
+                )
+            engine = nc.vector if t < 3 else nc.vector
+            for cols in ([slice(0, S)] if t < 3 else [slice(0, W), slice(W, S)]):
+                engine.tensor_tensor(res[:, cols], ub2[t][:, cols], sg[:, cols], ALU.mult)
+                nc.sync.dma_start(out_rows[t][:, cols], res[:, cols])
+
+        for t in range(4):
+            h2 = keep.tile([P, S], F32, name="h2_%d" % t)
+            for half in (1, 0):
+                nc.scalar.activation(h2[:, half * W : (half + 1) * W], h2_bank[t][half][:], ACT.Copy)
+            pa = keep.tile([P, W], F32, name="pa2_%d" % t)
+            pb = keep.tile([P, W], F32, name="pb2_%d" % t)
+            ra = keep.tile([P, W], F32, name="ra2_%d" % t)
+            rb = keep.tile([P, W], F32, name="rb2_%d" % t)
+            u = keep.tile([P, S], F32, name="ub2_%d" % t)
+            ub2.append(u)
+            piece = W // 2 if t == 0 else W
+            for first in range(0, W, piece):
+                cols = slice(first, first + piece)
+                nc.scalar.activation(pa[:, cols], h2[:].indirect(entries(n6_t, first, piece)), ACT.Copy)
+                nc.scalar.activation(pb[:, cols], h2[:].indirect(entries(n7_t, first, piece)), ACT.Copy)
+                nc.vector.tensor_tensor(ra[:, cols], pa[:, cols], pb[:, cols], ALU.max)
+                nc.vector.tensor_tensor(rb[:, cols], pa[:, cols], pb[:, cols], ALU.min)
+                nc.vector.tensor_copy(u[:].indirect(entries(n8_t, first, piece)), ra[:, cols])
+            if t > 0:
+                finish_out(t - 1)
+            nc.vector.tensor_copy(u[:].indirect(n9_t[:]), rb[:])
+
+        finish_out(3)

@@ -54,16 +54,16 @@ def tile_picked_mhhzntcphdeord_none_p_kernel(
 
         ds_win = keep.tile([P, G], U8, name="ds_win")
         xs_win = keep.tile([P, T], U8, name="xs_win")
-        k1_t = load_list("k1_t", k1)
-        nc.scalar.dma_start(ds_win[:].bitcast(I32), d_scales[0].bitcast(I32).unsqueeze(1).to_broadcast([16, 8, G // 4]))
-        nc.scalar.dma_start(xs_win[:].bitcast(I32), x_scales[0].bitcast(I32).unsqueeze(1).to_broadcast([16, 8, T // 4]))
-        k2_t = load_list("k2_t", k2)
         offs_t = load_list("offs_t", offs)
+        nc.scalar.dma_start(xs_win[:].bitcast(I32), x_scales[0].bitcast(I32).unsqueeze(1).to_broadcast([16, 8, T // 4]))
+        nc.scalar.dma_start(ds_win[:].bitcast(I32), d_scales[0].bitcast(I32).unsqueeze(1).to_broadcast([16, 8, G // 4]))
+        k1_t = load_list("k1_t", k1)
+        k2_t = load_list("k2_t", k2)
         hz_t = load_list("hz_t", hz)
-        xw_win = keep.tile([P, T], U32, name="xw_win")
-        nc.sync.dma_start(xw_win[:].bitcast(I32), x_words[0].rearrange("p n r -> p (n r)").bitcast(I32))
         dw_win = keep.tile([P, G], U32, name="dw_win")
         nc.sync.dma_start(dw_win[:].bitcast(I32), d_words[0].rearrange("p n r -> p (n r)").bitcast(I32))
+        xw_win = keep.tile([P, T], U32, name="xw_win")
+        nc.sync.dma_start(xw_win[:].bitcast(I32), x_words[0].rearrange("p n r -> p (n r)").bitcast(I32))
         n1_t = load_list("n1_t", n1)
         n2_t = load_list("n2_t", n2)
         n3_t = load_list("n3_t", n3)
@@ -80,33 +80,36 @@ def tile_picked_mhhzntcphdeord_none_p_kernel(
         n8_t = load_list("n8_t", n8)
         n9_t = load_list("n9_t", n9)
         n10_t = load_list("n10_t", n10)
+        gn_t = keep.tile([P, 4], F32, name="gn_t")
+        nc.gpsimd.dma_start(gn_t[:], gn.rearrange("(p t) o -> p (t o)", t=4))
+        neg_gn = keep.tile([P, 4], F32, name="neg_gn")
+        nc.scalar.activation(neg_gn[:], gn_t[:], ACT.Copy, scale=-1.0)
         for a, scales in enumerate((w1_scales, w2_scales)):
             for q in range(4):
                 nc.gpsimd.dma_start(
                     ws_raw[32 * q : 32 * q + 4, a * S : (a + 1) * S].bitcast(I32), scales[0, 4 * q : 4 * q + 4, :].bitcast(I32)
                 )
-        gn_t = keep.tile([P, 4], F32, name="gn_t")
-        sl_t = keep.tile([P, 4], F32, name="sl_t")
-        th_t = keep.tile([P, 4], F32, name="th_t")
-        for tile, src in ((gn_t, gn), (sl_t, sl), (th_t, th)):
-            nc.gpsimd.dma_start(tile[:], src.rearrange("(p t) o -> p (t o)", t=4))
-        neg_gn = keep.tile([P, 4], F32, name="neg_gn")
-        nc.gpsimd.tensor_scalar(neg_gn[:], gn_t[:], -1.0, 0.0, ALU.mult, ALU.add)
+        sl_t = keep.tile([P, 4, 8], F32, name="sl_t")
+        th_t = keep.tile([P, 4, 8], F32, name="th_t")
+        with nc.allow_non_contiguous_dma(reason="one value a row"):
+            for tile, src in ((sl_t, sl), (th_t, th)):
+                for t in range(4):
+                    nc.gpsimd.dma_start(tile[:, t, 0:1], src.rearrange("(a t q) o -> t a q o", t=4, q=4)[t])
         sl_th = keep.tile([P, 4], F32, name="sl_th")
-        nc.gpsimd.tensor_tensor(sl_th[:], sl_t[:], th_t[:], ALU.mult)
+        nc.gpsimd.tensor_tensor(sl_th[:], sl_t[:, :, 0], th_t[:, :, 0], ALU.mult)
         sg_bias = keep.tile([P, 4], F32, name="sg_bias")
         nc.gpsimd.tensor_scalar(sg_bias[:], sl_th[:], -1.0, 0.0, ALU.mult, ALU.add)
 
         ds_picked = keep.tile([P, 2, S], U8, name="ds_picked")
         xs_picked = keep.tile([P, 2, S], U8, name="xs_picked")
         ds_dealt = keep.tile([P, 2, 4, P], U8, name="ds_dealt")
+        nc.vector.tensor_copy(xs_picked[:, 0, :], xs_win[:].indirect(offs_t[:]))
         for a, lst in enumerate((k1_t, k2_t)):
             nc.vector.tensor_copy(ds_picked[:, a, :], ds_win[:].indirect(lst[:]))
-        nc.vector.tensor_copy(xs_picked[:, 0, :], xs_win[:].indirect(offs_t[:]))
-        nc.vector.tensor_copy(ds_dealt[:].rearrange("p a t m -> p a m t"), ds_picked[:].rearrange("p a (m t) -> p a m t", t=4))
-        place_scale_rows(d_s, ds_dealt[:].rearrange("p a t m -> p (a t m)"))
         nc.vector.tensor_copy(xs_picked[:, 1, :], xs_win[:].indirect(hz_t[:]))
         place_scale_rows(x_s, xs_picked[:].rearrange("p a c -> p (a c)"))
+        nc.vector.tensor_copy(ds_dealt[:].rearrange("p a t m -> p a m t"), ds_picked[:].rearrange("p a (m t) -> p a m t", t=4))
+        place_scale_rows(d_s, ds_dealt[:].rearrange("p a t m -> p (a t m)"))
 
         d_w, x_w = [], []
         for a, (d_lst, x_lst) in enumerate(((k1_t, offs_t), (k2_t, hz_t))):
@@ -120,8 +123,8 @@ def tile_picked_mhhzntcphdeord_none_p_kernel(
             d_w.append(dealt)
 
         h_bank = [psum.tile([P, S], F32, name="h_bank%d" % t, tag="bank") for t in range(4)]
-        for a in range(2):
-            for t in range(4):
+        for t, a in ((0, 0), (1, 0), (0, 1), (1, 1), (2, 0), (2, 1), (3, 0), (3, 1)):
+            if True:
                 nc.tensor.matmul_mx(
                     h_bank[t][:], lhsT=d_w[a][:, t, :].bitcast(FP8X4), lhsT_scale=d_s[:, a * S + t * P : a * S + (t + 1) * P],
                     rhs=x_w[a][:].bitcast(FP8X4), rhs_scale=x_s[:, a * S : (a + 1) * S],
@@ -129,115 +132,133 @@ def tile_picked_mhhzntcphdeord_none_p_kernel(
                 )
 
         two_picked = shared.tile([P, S], U8, name="two_picked", offset=4096 - 448, align_bytes=64)
-        w_s = shared.tile([P, 2, 4, P], U8, name="w_s", offset=4096 + 64, align_bytes=64)
-        two_w = shared.tile([P, S], U32, name="two_w", offset=4096 + 64 + 1024, align_bytes=64)
+        two_w = shared.tile([P, S], U32, name="two_w", offset=4096 + 64, align_bytes=64)
         nc.vector.tensor_copy(two_picked[:], xs_win[:].indirect(two_t[:]))
         place_scale_rows(two_s, two_picked)
         nc.vector.tensor_copy(two_w[:], xw_win[:].indirect(two_t[:]))
-        nc.vector.tensor_copy(w_s[:].rearrange("p a t m -> p a m t"), ws_raw[:].rearrange("p (a m t) -> p a m t", a=2, t=4))
         w_w = []
         for a in range(2):
             dealt = keep.tile([P, 4, 2 * P], U8, name="w_w%d" % a, align_bytes=64)
-            nc.scalar.copy(dealt[:].bitcast(U16), w_raw[a][:].bitcast(U16).rearrange("p (m t) -> p t m", t=4))
+            nc.scalar.copy(
+                dealt[:].bitcast(U32).rearrange("p t (a e) -> p t a e", e=2),
+                w_raw[a][:].bitcast(U32).rearrange("p (a t e) -> p t a e", t=4, e=2),
+            )
             w_w.append(dealt)
 
-        z_planes = keep.tile([P, 4, S], BF16, name="z_planes")
-        ub = []
+        ub = [keep.tile([P, S], F32, name="ub%d" % t) for t in range(4)]
+        pa = [shared.tile([P, 2, W], F32, name="pa%d" % g, offset=8192 + 4096 * g, align_bytes=64) for g in range(2)]
+        pb = [shared.tile([P, 2, W], F32, name="pb%d" % g, offset=8192 + 4096 * g + 2048, align_bytes=64) for g in range(2)]
+        rb = [keep.tile([P, 2, W], F32, name="rb%d" % g) for g in range(2)]
+        h = [shared.tile([P, S], F32, name="h%d" % t, offset=28672 + 2048 * t, align_bytes=64) for t in range(4)]
+        for g in range(2):
+            for t in (2 * g, 2 * g + 1):
+                nc.scalar.activation(h[t][:], h_bank[t][:], ACT.Copy, scale=0.0625)
+            for t in (2 * g, 2 * g + 1):
+                piece = W // 2 if t == 0 else W
+                for first in range(0, W, piece):
+                    cols = slice(first, first + piece)
+                    nc.scalar.activation(pa[g][:, t % 2, cols], h[t][:].indirect(entries(n1_t, first, piece)), ACT.Copy)
+                    nc.scalar.activation(pb[g][:, t % 2, cols], h[t][:].indirect(entries(n2_t, first, piece)), ACT.Copy)
+        w_s = shared.tile([P, 2, 4, P], U8, name="w_s", offset=28672 + 2048, align_bytes=64)
+        nc.scalar.copy(w_s[:].bitcast(U32), ws_raw[:].bitcast(U32).rearrange("p (b a t) -> p b t a", b=2, t=4))
 
-        def finish_z(t):
-            scaled = keep.tile([P, S], F32, name="scaled%d" % t)
-            far = keep.tile([P, S], F32, name="far%d" % t)
-            nc.scalar.activation(scaled[:], ub[t][:], ACT.Copy, scale=gn_t[:, t : t + 1])
-            for first in (0, W):
-                nc.scalar.activation(far[:, first : first + W], scaled[:].indirect(entries(n5_t, first, W)), ACT.Copy)
-            nc.vector.tensor_tensor(z_planes[:, t, :], scaled[:], far[:], ALU.subtract)
+        def put_sum(t, first, count):
+            cols = slice(first, first + count)
+            nc.vector.tensor_tensor(
+                ub[t][:].indirect(entries(n3_t, first, count)), pa[t // 2][:, t % 2, cols], pb[t // 2][:, t % 2, cols], ALU.add
+            )
 
-        for t in range(4):
-            h = keep.tile([P, S], F32, name="h%d" % t)
-            nc.scalar.activation(h[:], h_bank[t][:], ACT.Copy, scale=0.0625)
-            pa = keep.tile([P, W], F32, name="pa%d" % t)
-            pb = keep.tile([P, W], F32, name="pb%d" % t)
-            rb = keep.tile([P, W], F32, name="rb%d" % t)
-            u = keep.tile([P, S], F32, name="ub%d" % t)
-            ub.append(u)
-            piece = W // 2 if t == 0 else W
+        for g in range(2):
+            piece = W // 2 if g == 0 else W
             for first in range(0, W, piece):
-                cols = slice(first, first + piece)
-                nc.scalar.activation(pa[:, cols], h[:].indirect(entries(n1_t, first, piece)), ACT.Copy)
-                nc.scalar.activation(pb[:, cols], h[:].indirect(entries(n2_t, first, piece)), ACT.Copy)
-                nc.vector.tensor_tensor(u[:].indirect(entries(n3_t, first, piece)), pa[:, cols], pb[:, cols], ALU.add)
-                nc.vector.tensor_tensor(rb[:, cols], pa[:, cols], pb[:, cols], ALU.max)
-            if t > 0:
-                finish_z(t - 1)
-            nc.vector.tensor_copy(u[:].indirect(n4_t[:]), rb[:])
+                put_sum(2 * g, first, piece)
+            nc.vector.tensor_tensor(rb[g][:], pa[g][:], pb[g][:], ALU.max)
+            put_sum(2 * g + 1, 0, W)
+            for i in range(2):
+                nc.vector.tensor_copy(ub[2 * g + i][:].indirect(n4_t[:]), rb[g][:, i, :])
 
-        scaled = keep.tile([P, S], F32, name="scaled3")
-        far = keep.tile([P, S], F32, name="far3")
-        nc.vector.tensor_scalar(scaled[:], ub[3][:], gn_t[:, 3:4], None, ALU.mult)
-        for first in (0, W):
-            cols = slice(first, first + W)
-            nc.scalar.activation(far[:, cols], ub[3][:].indirect(entries(n5_t, first, W)), ACT.Copy)
-            nc.vector.scalar_tensor_tensor(z_planes[:, 3, cols], far[:, cols], neg_gn[:, 3:4], scaled[:, cols], ALU.mult, ALU.add)
+        z_planes = shared.tile([P, 4, S], BF16, name="z_planes", offset=8192 + 4096, align_bytes=64)
+        scaled = [shared.tile([P, S], F32, name="scaled%d" % t, offset=33792 + 2048 * t if t < 2 else 57344 + 2048 * t, align_bytes=64) for t in range(4)]
+        far = [shared.tile([P, S], F32, name="far%d" % t, offset=(53248, 55296, 33792, 53248)[t], align_bytes=64) for t in range(4)]
+        for t in range(2):
+            nc.scalar.activation(scaled[t][:], ub[t][:], ACT.Copy, scale=gn_t[:, t : t + 1])
+            for first in (0, W):
+                nc.scalar.activation(far[t][:, first : first + W], scaled[t][:].indirect(entries(n5_t, first, W)), ACT.Copy)
+            nc.gpsimd.tensor_tensor(z_planes[:, t, :], scaled[t][:], far[t][:], ALU.subtract)
+        for t in (2, 3):
+            for first in (0, W):
+                nc.scalar.activation(far[t][:, first : first + W], ub[t][:].indirect(entries(n5_t, first, W)), ACT.Copy)
+        for t in (2, 3):
+            nc.vector.tensor_scalar(scaled[t][:], ub[t][:], gn_t[:, t : t + 1], None, ALU.mult)
+        for t, cols in ((2, slice(0, S)), (3, slice(0, W)), (3, slice(W, S))):
+            nc.vector.scalar_tensor_tensor(
+                z_planes[:, t, cols], far[t][:, cols], neg_gn[:, t : t + 1], scaled[t][:, cols], ALU.mult, ALU.add
+            )
         grouped = [keep.tile([P, W, 4], BF16, name="grouped%d" % half, align_bytes=64) for half in range(2)]
-        nc.scalar.copy(grouped[0][:], z_planes[:, :, 0:W].rearrange("p t c -> p c t"))
-        nc.vector.tensor_copy(grouped[1][:], z_planes[:, :, W:S].rearrange("p t c -> p c t"))
-        z_w = [keep.tile([P, W], U32, name="z_w%d" % half, align_bytes=64) for half in range(2)]
-        z_s = [keep.tile([P, W], U8, name="z_s%d" % half, align_bytes=64) for half in range(2)]
-        for half in (1, 0):
-            nc.vector.quantize_mx(z_w[half][:].bitcast(FP8X4), z_s[half][:], grouped[half][:].rearrange("p c t -> p (c t)"))
+        nc.vector.tensor_copy(grouped[0][:], z_planes[:, :, 0:W].rearrange("p t c -> p c t"))
+        nc.scalar.copy(grouped[1][:], z_planes[:, :, W:S].rearrange("p t c -> p c t"))
+        z_w = keep.tile([P, S], U32, name="z_w", align_bytes=64)
+        z_s = keep.tile([P, S], U8, name="z_s", align_bytes=64)
+        for half in range(2):
+            cols = slice(half * W, (half + 1) * W)
+            nc.vector.quantize_mx(z_w[:, cols].bitcast(FP8X4), z_s[:, cols], grouped[half][:].rearrange("p c t -> p (c t)"))
 
-        h2_bank = [[psum.tile([P, W], F32, name="h2_bank%d_%d" % (t, half), tag="bank") for half in range(2)] for t in range(4)]
-        for t in range(4):
-            for half in range(2):
+        spans = [(0, slice(0, W)), (0, slice(W, S)), (1, slice(0, S)), (2, slice(0, S)), (3, slice(0, S))]
+        h2_bank = [psum.tile([P, cols.stop - cols.start], F32, name="h2_bank%d" % b, tag="bank") for b, (t, cols) in enumerate(spans)]
+        for a, (words, scales) in ((1, (two_w, two_s)), (0, (z_w, z_s))):
+            for b, (t, cols) in enumerate(spans):
                 nc.tensor.matmul_mx(
-                    h2_bank[t][half][:], lhsT=w_w[1][:, t, :].bitcast(FP4X4), lhsT_scale=w_s[:, 1, t, :],
-                    rhs=two_w[:, half * W : (half + 1) * W].bitcast(FP8X4), rhs_scale=two_s[:, half * W : (half + 1) * W],
-                    start=True, stop=False,
-                )
-        for t in range(4):
-            for half in (1, 0):
-                nc.tensor.matmul_mx(
-                    h2_bank[t][half][:], lhsT=w_w[0][:, t, :].bitcast(FP4X4), lhsT_scale=w_s[:, 0, t, :],
-                    rhs=z_w[half][:].bitcast(FP8X4), rhs_scale=z_s[half][:],
-                    start=False, stop=True,
+                    h2_bank[b][:], lhsT=w_w[a][:, t, :].bitcast(FP4X4), lhsT_scale=w_s[:, a, t, :],
+                    rhs=words[:, cols].bitcast(FP8X4), rhs_scale=scales[:, cols],
+                    start=(a == 1), stop=(a == 0),
                 )
 
-        out_rows = out.rearrange("(p t) j -> t p j", t=4)
-        ub2 = []
-
-        def finish_out(t):
-            sg = keep.tile([P, S], F32, name="sg%d" % t)
-            res = keep.tile([P, S], F32, name="res%d" % t)
-            for first in (0, W):
+        out_rows = out.rearrange("(a t q) j -> t a q j", t=4, q=4)
+        ub2 = [keep.tile([P, S], F32, name="ub2_%d" % t) for t in range(4)]
+        pa2 = [shared.tile([P, 2, W], F32, name="pa2_%d" % g, offset=20480 + 4096 * g, align_bytes=64) for g in range(2)]
+        pb2 = [shared.tile([P, 2, W], F32, name="pb2_%d" % g, offset=20480 + 4096 * g + 2048, align_bytes=64) for g in range(2)]
+        ra2 = [keep.tile([P, 2, W], F32, name="ra2_%d" % g) for g in range(2)]
+        rb2 = [keep.tile([P, 2, W], F32, name="rb2_%d" % g) for g in range(2)]
+        h2 = [shared.tile([P, S], F32, name="h2_%d" % t, offset=38912 + 2048 * t, align_bytes=64) for t in range(4)]
+        nc.vector.tensor_copy(h2[1][:], h2_bank[2][:])
+        for g, banks in enumerate(((0, 1), (3, 4))):
+            for b in banks:
+                t, cols = spans[b]
+                nc.scalar.activation(h2[t][:, cols], h2_bank[b][:], ACT.Copy)
+            for t in (2 * g, 2 * g + 1):
+                piece = W // 2 if t == 0 else W
+                for first in range(0, W, piece):
+                    cols = slice(first, first + piece)
+                    nc.scalar.activation(pa2[g][:, t % 2, cols], h2[t][:].indirect(entries(n6_t, first, piece)), ACT.Copy)
+                    nc.scalar.activation(pb2[g][:, t % 2, cols], h2[t][:].indirect(entries(n7_t, first, piece)), ACT.Copy)
+        for first in (0, W // 2):
+            cols = slice(first, first + W // 2)
+            nc.vector.tensor_tensor(ra2[0][:, 0, cols], pa2[0][:, 0, cols], pb2[0][:, 0, cols], ALU.max)
+            nc.vector.tensor_copy(ub2[0][:].indirect(entries(n8_t, first, W // 2)), ra2[0][:, 0, cols])
+        nc.vector.tensor_tensor(ra2[0][:, 1, :], pa2[0][:, 1, :], pb2[0][:, 1, :], ALU.max)
+        nc.vector.tensor_tensor(rb2[0][:], pa2[0][:], pb2[0][:], ALU.min)
+        nc.vector.tensor_copy(ub2[1][:].indirect(n8_t[:]), ra2[0][:, 1, :])
+        for i in range(2):
+            nc.vector.tensor_copy(ub2[i][:].indirect(n9_t[:]), rb2[0][:, i, :])
+        nc.vector.tensor_tensor(ra2[1][:], pa2[1][:], pb2[1][:], ALU.max)
+        nc.vector.tensor_tensor(rb2[1][:], pa2[1][:], pb2[1][:], ALU.min)
+        for lst, values in ((n8_t, ra2[1]), (n9_t, rb2[1])):
+            for i in range(2):
+                nc.vector.tensor_copy(ub2[2 + i][:].indirect(lst[:]), values[:, i, :])
+        for t in range(4):
+            sg = shared.tile([P, S], F32, name="sg%d" % t, offset=38912 + 5120 + 2048 * t, align_bytes=64)
+            if t < 2:
+                res = shared.tile([P, S], F32, name="res%d" % t, offset=24576 + 2048 * t, align_bytes=64)
+            else:
+                res = keep.tile([P, S], F32, name="res%d" % t)
+            pieces = [(0, W), (W, W)] if t < 3 else [(0, W), (W, W // 2), (W + W // 2, W // 2)]
+            for first, count in pieces:
                 nc.scalar.activation(
-                    sg[:, first : first + W], ub2[t][:].indirect(entries(n10_t, first, W)), ACT.Sigmoid,
-                    scale=sl_t[:, t : t + 1], bias=sg_bias[:, t : t + 1],
+                    sg[:, first : first + count], ub2[t][:].indirect(entries(n10_t, first, count)), ACT.Sigmoid,
+                    scale=sl_t[:, t, 0:1], bias=sg_bias[:, t : t + 1],
                 )
-            engine = nc.vector if t < 3 else nc.vector
-            for cols in ([slice(0, S)] if t < 3 else [slice(0, W), slice(W, S)]):
+            engine = nc.gpsimd if t < 2 else nc.vector
+            for first, count in ([(0, S)] if t < 3 else pieces):
+                cols = slice(first, first + count)
                 engine.tensor_tensor(res[:, cols], ub2[t][:, cols], sg[:, cols], ALU.mult)
-                nc.sync.dma_start(out_rows[t][:, cols], res[:, cols])
-
-        for t in range(4):
-            h2 = keep.tile([P, S], F32, name="h2_%d" % t)
-            for half in (1, 0):
-                nc.scalar.activation(h2[:, half * W : (half + 1) * W], h2_bank[t][half][:], ACT.Copy)
-            pa = keep.tile([P, W], F32, name="pa2_%d" % t)
-            pb = keep.tile([P, W], F32, name="pb2_%d" % t)
-            ra = keep.tile([P, W], F32, name="ra2_%d" % t)
-            rb = keep.tile([P, W], F32, name="rb2_%d" % t)
-            u = keep.tile([P, S], F32, name="ub2_%d" % t)
-            ub2.append(u)
-            piece = W // 2 if t == 0 else W
-            for first in range(0, W, piece):
-                cols = slice(first, first + piece)
-                nc.scalar.activation(pa[:, cols], h2[:].indirect(entries(n6_t, first, piece)), ACT.Copy)
-                nc.scalar.activation(pb[:, cols], h2[:].indirect(entries(n7_t, first, piece)), ACT.Copy)
-                nc.vector.tensor_tensor(ra[:, cols], pa[:, cols], pb[:, cols], ALU.max)
-                nc.vector.tensor_tensor(rb[:, cols], pa[:, cols], pb[:, cols], ALU.min)
-                nc.vector.tensor_copy(u[:].indirect(entries(n8_t, first, piece)), ra[:, cols])
-            if t > 0:
-                finish_out(t - 1)
-            nc.vector.tensor_copy(u[:].indirect(n9_t[:]), rb[:])
-
-        finish_out(3)
+                nc.sync.dma_start(out_rows[t][:, :, cols], res[:, cols])

@@ -14,8 +14,19 @@ ALU = mybir.AluOpType
 ACT = mybir.ActivationFunctionType
 
 P = 128
-T, G, S, W = 1024, 2048, 512, 256
+T, G = 1024, 2048
+S = 512
+W = 256
+LEAD = 128
 FLOPS = 4 * 2 * 512 * 512 * 512
+
+ROW = 4 * S
+AT_D_PICKED = 0
+AT_PAIRS = 4 * ROW
+AT_PAIRS2 = 10 * ROW
+AT_H = 14 * ROW
+AT_H2 = 19 * ROW
+AT_FAR = 26 * ROW
 
 
 def entries(lst, first, count):
@@ -38,7 +49,7 @@ def tile_picked_mhhzntcphdeord_none_p_kernel(
             nc.sync.dma_start(tile[:], src)
             return tile
 
-        def zeroed_bytes(name, width, engine):
+        def scale_operand(name, width, engine):
             tile = keep.tile([P, width], U8, name=name, align_bytes=64)
             engine.memset(tile[:].bitcast(I32), 0)
             return tile
@@ -47,10 +58,13 @@ def tile_picked_mhhzntcphdeord_none_p_kernel(
             for q in range(4):
                 nc.sync.dma_start(dst[32 * q : 32 * q + 4, :].bitcast(I32), src[32 * q : 32 * q + 32 : 8, :].bitcast(I32))
 
-        ws_raw = zeroed_bytes("ws_raw", 2 * S, nc.gpsimd)
-        d_s = zeroed_bytes("d_s", 2 * S, nc.vector)
-        x_s = zeroed_bytes("x_s", 2 * S, nc.vector)
-        two_s = zeroed_bytes("two_s", S, nc.vector)
+        def placed(name, shape, dtype, offset):
+            return shared.tile(shape, dtype, name=name, offset=offset, align_bytes=64)
+
+        ws_raw = scale_operand("ws_raw", 2 * S, nc.gpsimd)
+        d_s = scale_operand("d_s", 2 * S, nc.vector)
+        x_s = scale_operand("x_s", 2 * S, nc.vector)
+        two_s = scale_operand("two_s", S, nc.vector)
 
         ds_win = keep.tile([P, G], U8, name="ds_win")
         xs_win = keep.tile([P, T], U8, name="xs_win")
@@ -113,7 +127,7 @@ def tile_picked_mhhzntcphdeord_none_p_kernel(
 
         d_w, x_w = [], []
         for a, (d_lst, x_lst) in enumerate(((k1_t, offs_t), (k2_t, hz_t))):
-            picked = shared.tile([P, S], U32, name="dw_picked%d" % a, offset=4096 * a, align_bytes=64)
+            picked = placed("dw_picked%d" % a, [P, S], U32, AT_D_PICKED + 2 * ROW * a)
             nc.vector.tensor_copy(picked[:], dw_win[:].indirect(d_lst[:]))
             xw = keep.tile([P, S], U32, name="x_w%d" % a, align_bytes=64)
             nc.vector.tensor_copy(xw[:], xw_win[:].indirect(x_lst[:]))
@@ -123,16 +137,16 @@ def tile_picked_mhhzntcphdeord_none_p_kernel(
             d_w.append(dealt)
 
         h_bank = [psum.tile([P, S], F32, name="h_bank%d" % t, tag="bank") for t in range(4)]
-        for t, a in ((0, 0), (1, 0), (0, 1), (1, 1), (2, 0), (2, 1), (3, 0), (3, 1)):
-            if True:
-                nc.tensor.matmul_mx(
-                    h_bank[t][:], lhsT=d_w[a][:, t, :].bitcast(FP8X4), lhsT_scale=d_s[:, a * S + t * P : a * S + (t + 1) * P],
-                    rhs=x_w[a][:].bitcast(FP8X4), rhs_scale=x_s[:, a * S : (a + 1) * S],
-                    start=(a == 0), stop=(a == 1),
-                )
+        passes = [(t, a) for a in range(2) for t in (0, 1)] + [(t, a) for t in (2, 3) for a in range(2)]
+        for t, a in passes:
+            nc.tensor.matmul_mx(
+                h_bank[t][:], lhsT=d_w[a][:, t, :].bitcast(FP8X4), lhsT_scale=d_s[:, a * S + t * P : a * S + (t + 1) * P],
+                rhs=x_w[a][:].bitcast(FP8X4), rhs_scale=x_s[:, a * S : (a + 1) * S],
+                start=(a == 0), stop=(a == 1),
+            )
 
-        two_picked = shared.tile([P, S], U8, name="two_picked", offset=4096 - 448, align_bytes=64)
-        two_w = shared.tile([P, S], U32, name="two_w", offset=4096 + 64, align_bytes=64)
+        two_picked = placed("two_picked", [P, S], U8, AT_D_PICKED + 2 * ROW + 64 - S)
+        two_w = placed("two_w", [P, S], U32, AT_D_PICKED + 2 * ROW + 64)
         nc.vector.tensor_copy(two_picked[:], xs_win[:].indirect(two_t[:]))
         place_scale_rows(two_s, two_picked)
         nc.vector.tensor_copy(two_w[:], xw_win[:].indirect(two_t[:]))
@@ -146,20 +160,20 @@ def tile_picked_mhhzntcphdeord_none_p_kernel(
             w_w.append(dealt)
 
         ub = [keep.tile([P, S], F32, name="ub%d" % t) for t in range(4)]
-        pa = [shared.tile([P, 2, W], F32, name="pa%d" % g, offset=8192 + 4096 * g, align_bytes=64) for g in range(2)]
-        pb = [shared.tile([P, 2, W], F32, name="pb%d" % g, offset=8192 + 4096 * g + 2048, align_bytes=64) for g in range(2)]
+        pa = [placed("pa%d" % g, [P, 2, W], F32, AT_PAIRS + 2 * ROW * g) for g in range(2)]
+        pb = [placed("pb%d" % g, [P, 2, W], F32, AT_PAIRS + 2 * ROW * g + ROW) for g in range(2)]
         rb = [keep.tile([P, 2, W], F32, name="rb%d" % g) for g in range(2)]
-        h = [shared.tile([P, S], F32, name="h%d" % t, offset=28672 + 2048 * t, align_bytes=64) for t in range(4)]
+        h = [placed("h%d" % t, [P, S], F32, AT_H + ROW * t) for t in range(4)]
         for g in range(2):
             for t in (2 * g, 2 * g + 1):
                 nc.scalar.activation(h[t][:], h_bank[t][:], ACT.Copy, scale=0.0625)
             for t in (2 * g, 2 * g + 1):
-                piece = W // 2 if t == 0 else W
+                piece = LEAD if t == 0 else W
                 for first in range(0, W, piece):
                     cols = slice(first, first + piece)
                     nc.scalar.activation(pa[g][:, t % 2, cols], h[t][:].indirect(entries(n1_t, first, piece)), ACT.Copy)
                     nc.scalar.activation(pb[g][:, t % 2, cols], h[t][:].indirect(entries(n2_t, first, piece)), ACT.Copy)
-        w_s = shared.tile([P, 2, 4, P], U8, name="w_s", offset=28672 + 2048, align_bytes=64)
+        w_s = placed("w_s", [P, 2, 4, P], U8, AT_H + ROW)
         nc.scalar.copy(w_s[:].bitcast(U32), ws_raw[:].bitcast(U32).rearrange("p (b a t) -> p b t a", b=2, t=4))
 
         def put_sum(t, first, count):
@@ -169,7 +183,7 @@ def tile_picked_mhhzntcphdeord_none_p_kernel(
             )
 
         for g in range(2):
-            piece = W // 2 if g == 0 else W
+            piece = LEAD if g == 0 else W
             for first in range(0, W, piece):
                 put_sum(2 * g, first, piece)
             nc.vector.tensor_tensor(rb[g][:], pa[g][:], pb[g][:], ALU.max)
@@ -177,14 +191,16 @@ def tile_picked_mhhzntcphdeord_none_p_kernel(
             for i in range(2):
                 nc.vector.tensor_copy(ub[2 * g + i][:].indirect(n4_t[:]), rb[g][:, i, :])
 
-        z_planes = shared.tile([P, 4, S], BF16, name="z_planes", offset=8192 + 4096, align_bytes=64)
-        scaled = [shared.tile([P, S], F32, name="scaled%d" % t, offset=33792 + 2048 * t if t < 2 else 57344 + 2048 * t, align_bytes=64) for t in range(4)]
-        far = [shared.tile([P, S], F32, name="far%d" % t, offset=(53248, 55296, 33792, 53248)[t], align_bytes=64) for t in range(4)]
+        z_tiles = placed("z_tiles", [P, 4, S], BF16, AT_PAIRS + 2 * ROW)
+        at_scaled = AT_H + 2 * ROW + ROW // 2
+        scaled = [placed("scaled%d" % t, [P, S], F32, at_scaled + ROW * t) for t in range(2)]
+        scaled.extend(keep.tile([P, S], F32, name="scaled%d" % t) for t in (2, 3))
+        far = [placed("far%d" % t, [P, S], F32, at) for t, at in enumerate((AT_FAR, AT_FAR + ROW, at_scaled, AT_FAR))]
         for t in range(2):
             nc.scalar.activation(scaled[t][:], ub[t][:], ACT.Copy, scale=gn_t[:, t : t + 1])
             for first in (0, W):
                 nc.scalar.activation(far[t][:, first : first + W], scaled[t][:].indirect(entries(n5_t, first, W)), ACT.Copy)
-            nc.gpsimd.tensor_tensor(z_planes[:, t, :], scaled[t][:], far[t][:], ALU.subtract)
+            nc.gpsimd.tensor_tensor(z_tiles[:, t, :], scaled[t][:], far[t][:], ALU.subtract)
         for t in (2, 3):
             for first in (0, W):
                 nc.scalar.activation(far[t][:, first : first + W], ub[t][:].indirect(entries(n5_t, first, W)), ACT.Copy)
@@ -192,11 +208,15 @@ def tile_picked_mhhzntcphdeord_none_p_kernel(
             nc.vector.tensor_scalar(scaled[t][:], ub[t][:], gn_t[:, t : t + 1], None, ALU.mult)
         for t, cols in ((2, slice(0, S)), (3, slice(0, W)), (3, slice(W, S))):
             nc.vector.scalar_tensor_tensor(
-                z_planes[:, t, cols], far[t][:, cols], neg_gn[:, t : t + 1], scaled[t][:, cols], ALU.mult, ALU.add
+                z_tiles[:, t, cols], far[t][:, cols], neg_gn[:, t : t + 1], scaled[t][:, cols], ALU.mult, ALU.add
             )
+
         grouped = [keep.tile([P, W, 4], BF16, name="grouped%d" % half, align_bytes=64) for half in range(2)]
-        nc.vector.tensor_copy(grouped[0][:], z_planes[:, :, 0:W].rearrange("p t c -> p c t"))
-        nc.scalar.copy(grouped[1][:], z_planes[:, :, W:S].rearrange("p t c -> p c t"))
+        for half, copy in enumerate((nc.vector.tensor_copy, nc.scalar.copy)):
+            copy(
+                grouped[half][:].rearrange("p (c i) t -> p c t i", i=4),
+                z_tiles[:, :, half * W : (half + 1) * W].rearrange("p t (c i) -> p c t i", i=4),
+            )
         z_w = keep.tile([P, S], U32, name="z_w", align_bytes=64)
         z_s = keep.tile([P, S], U8, name="z_s", align_bytes=64)
         for half in range(2):
@@ -215,28 +235,32 @@ def tile_picked_mhhzntcphdeord_none_p_kernel(
 
         out_rows = out.rearrange("(a t q) j -> t a q j", t=4, q=4)
         ub2 = [keep.tile([P, S], F32, name="ub2_%d" % t) for t in range(4)]
-        pa2 = [shared.tile([P, 2, W], F32, name="pa2_%d" % g, offset=20480 + 4096 * g, align_bytes=64) for g in range(2)]
-        pb2 = [shared.tile([P, 2, W], F32, name="pb2_%d" % g, offset=20480 + 4096 * g + 2048, align_bytes=64) for g in range(2)]
+        pa2 = [placed("pa2_%d" % g, [P, 2, W], F32, AT_PAIRS2 + 2 * ROW * g) for g in range(2)]
+        pb2 = [placed("pb2_%d" % g, [P, 2, W], F32, AT_PAIRS2 + 2 * ROW * g + ROW) for g in range(2)]
         ra2 = [keep.tile([P, 2, W], F32, name="ra2_%d" % g) for g in range(2)]
         rb2 = [keep.tile([P, 2, W], F32, name="rb2_%d" % g) for g in range(2)]
-        h2 = [shared.tile([P, S], F32, name="h2_%d" % t, offset=38912 + 2048 * t, align_bytes=64) for t in range(4)]
-        nc.vector.tensor_copy(h2[1][:], h2_bank[2][:])
-        for g, banks in enumerate(((0, 1), (3, 4))):
+        h2 = [placed("h2_%d" % t, [P, S], F32, AT_H2 + ROW * t) for t in range(4)]
+        for b in (1, 2):
+            t, cols = spans[b]
+            nc.vector.tensor_copy(h2[t][:, cols], h2_bank[b][:])
+        for g, banks in enumerate(((0,), (3, 4))):
             for b in banks:
                 t, cols = spans[b]
                 nc.scalar.activation(h2[t][:, cols], h2_bank[b][:], ACT.Copy)
             for t in (2 * g, 2 * g + 1):
-                piece = W // 2 if t == 0 else W
+                piece = LEAD if t == 0 else W
                 for first in range(0, W, piece):
                     cols = slice(first, first + piece)
                     nc.scalar.activation(pa2[g][:, t % 2, cols], h2[t][:].indirect(entries(n6_t, first, piece)), ACT.Copy)
                     nc.scalar.activation(pb2[g][:, t % 2, cols], h2[t][:].indirect(entries(n7_t, first, piece)), ACT.Copy)
-        for first in (0, W // 2):
-            cols = slice(first, first + W // 2)
-            nc.vector.tensor_tensor(ra2[0][:, 0, cols], pa2[0][:, 0, cols], pb2[0][:, 0, cols], ALU.max)
-            nc.vector.tensor_copy(ub2[0][:].indirect(entries(n8_t, first, W // 2)), ra2[0][:, 0, cols])
+        flat_a, flat_b, flat_min = (x[:].rearrange("p i c -> p (i c)") for x in (pa2[0], pb2[0], rb2[0]))
+        nc.vector.tensor_tensor(ra2[0][:, 0, 0:LEAD], pa2[0][:, 0, 0:LEAD], pb2[0][:, 0, 0:LEAD], ALU.max)
+        nc.vector.tensor_tensor(flat_min[:, 0:LEAD], flat_a[:, 0:LEAD], flat_b[:, 0:LEAD], ALU.min)
+        nc.vector.tensor_copy(ub2[0][:].indirect(entries(n8_t, 0, LEAD)), ra2[0][:, 0, 0:LEAD])
+        nc.vector.tensor_tensor(ra2[0][:, 0, LEAD:W], pa2[0][:, 0, LEAD:W], pb2[0][:, 0, LEAD:W], ALU.max)
+        nc.vector.tensor_copy(ub2[0][:].indirect(entries(n8_t, LEAD, W - LEAD)), ra2[0][:, 0, LEAD:W])
         nc.vector.tensor_tensor(ra2[0][:, 1, :], pa2[0][:, 1, :], pb2[0][:, 1, :], ALU.max)
-        nc.vector.tensor_tensor(rb2[0][:], pa2[0][:], pb2[0][:], ALU.min)
+        nc.vector.tensor_tensor(flat_min[:, LEAD:], flat_a[:, LEAD:], flat_b[:, LEAD:], ALU.min)
         nc.vector.tensor_copy(ub2[1][:].indirect(n8_t[:]), ra2[0][:, 1, :])
         for i in range(2):
             nc.vector.tensor_copy(ub2[i][:].indirect(n9_t[:]), rb2[0][:, i, :])
@@ -245,13 +269,14 @@ def tile_picked_mhhzntcphdeord_none_p_kernel(
         for lst, values in ((n8_t, ra2[1]), (n9_t, rb2[1])):
             for i in range(2):
                 nc.vector.tensor_copy(ub2[2 + i][:].indirect(lst[:]), values[:, i, :])
+
         for t in range(4):
-            sg = shared.tile([P, S], F32, name="sg%d" % t, offset=38912 + 5120 + 2048 * t, align_bytes=64)
+            sg = placed("sg%d" % t, [P, S], F32, AT_H2 + 2 * ROW + ROW // 2 + ROW * t)
             if t < 2:
-                res = shared.tile([P, S], F32, name="res%d" % t, offset=24576 + 2048 * t, align_bytes=64)
+                res = placed("res%d" % t, [P, S], F32, AT_PAIRS2 + 2 * ROW + ROW * t)
             else:
                 res = keep.tile([P, S], F32, name="res%d" % t)
-            pieces = [(0, W), (W, W)] if t < 3 else [(0, W), (W, W // 2), (W + W // 2, W // 2)]
+            pieces = [(0, W), (W, W)] if t < 3 else [(0, W), (W, LEAD), (W + LEAD, LEAD)]
             for first, count in pieces:
                 nc.scalar.activation(
                     sg[:, first : first + count], ub2[t][:].indirect(entries(n10_t, first, count)), ACT.Sigmoid,

from contextlib import ExitStack

import concourse.mybir as mybir

F32 = mybir.dt.float32
BF16 = mybir.dt.bfloat16
I32 = mybir.dt.int32
U32 = mybir.dt.uint32
U16 = mybir.dt.uint16
U8 = mybir.dt.uint8
FP8X4 = mybir.dt.float8_e4m3fn_x4
FP4X4 = mybir.dt.float4_e2m1fn_x4
ALU = mybir.AluOpType
ACT = mybir.ActivationFunctionType

P = 128
T, G = 1024, 2048
S = 512
W = 256
LEAD = 128
FLOPS = 4 * 2 * 512 * 512 * 512

ROW = 4 * S
AT_D_PICKED = 0
AT_PAIRS = 4 * ROW
AT_PAIRS2 = 10 * ROW
AT_H = 14 * ROW
AT_H2 = 19 * ROW
AT_FAR = 26 * ROW


def entries(lst, first, count):
    return lst[:, first // 16 : (first + count) // 16]


def tile_picked_mhhzntcphdeord_none_p_kernel(
    tc, x_words, x_scales, d_words, d_scales, gn, w1_words, w1_scales, w2_words, w2_scales, sl, th,
    offs, k1, hz, k2, n1, n2, n3, n4, n5, two, n6, n7, n8, n9, n10, out,
):
    nc = tc.nc
    with ExitStack() as ctx:
        lists = ctx.enter_context(tc.tile_pool(name="lists", bufs=1))
        keep = ctx.enter_context(tc.tile_pool(name="keep", bufs=1))
        shared = ctx.enter_context(tc.tile_pool(name="shared", bufs=1))
        psum = ctx.enter_context(tc.psum_pool(name="psum", bufs=8))

        def load_list(name, src):
            tile = lists.tile([P, src.shape[1]], U16, name=name)
            nc.sync.dma_start(tile[:], src)
            return tile

        def scale_operand(name, width, engine):
            tile = keep.tile([P, width], U8, name=name, align_bytes=64)
            engine.memset(tile[:].bitcast(I32), 0)
            return tile

        def place_scale_rows(dst, src):
            for q in range(4):
                nc.sync.dma_start(dst[32 * q : 32 * q + 4, :].bitcast(I32), src[32 * q : 32 * q + 32 : 8, :].bitcast(I32))

        def placed(name, shape, dtype, offset):
            return shared.tile(shape, dtype, name=name, offset=offset, align_bytes=64)

        ws_raw = scale_operand("ws_raw", 2 * S, nc.gpsimd)
        d_s = scale_operand("d_s", 2 * S, nc.vector)
        x_s = scale_operand("x_s", 2 * S, nc.vector)
        two_s = scale_operand("two_s", S, nc.vector)

        ds_win = keep.tile([P, G], U8, name="ds_win")
        xs_win = keep.tile([P, T], U8, name="xs_win")
        offs_t = load_list("offs_t", offs)
        nc.scalar.dma_start(xs_win[:].bitcast(I32), x_scales[0].bitcast(I32).unsqueeze(1).to_broadcast([16, 8, T // 4]))
        nc.scalar.dma_start(ds_win[:].bitcast(I32), d_scales[0].bitcast(I32).unsqueeze(1).to_broadcast([16, 8, G // 4]))
        k1_t = load_list("k1_t", k1)
        k2_t = load_list("k2_t", k2)
        hz_t = load_list("hz_t", hz)
        dw_win = keep.tile([P, G], U32, name="dw_win")
        nc.sync.dma_start(dw_win[:].bitcast(I32), d_words[0].rearrange("p n r -> p (n r)").bitcast(I32))
        xw_win = keep.tile([P, T], U32, name="xw_win")
        nc.sync.dma_start(xw_win[:].bitcast(I32), x_words[0].rearrange("p n r -> p (n r)").bitcast(I32))
        n1_t = load_list("n1_t", n1)
        n2_t = load_list("n2_t", n2)
        n3_t = load_list("n3_t", n3)
        two_t = load_list("two_t", two)
        n4_t = load_list("n4_t", n4)
        n5_t = load_list("n5_t", n5)
        w_raw = []
        for a, words in enumerate((w1_words, w2_words)):
            raw = keep.tile([P, 2 * S], U8, name="w_raw%d" % a)
            nc.sync.dma_start(raw[:].bitcast(I32), words[0].bitcast(I32))
            w_raw.append(raw)
        n6_t = load_list("n6_t", n6)
        n7_t = load_list("n7_t", n7)
        n8_t = load_list("n8_t", n8)
        n9_t = load_list("n9_t", n9)
        n10_t = load_list("n10_t", n10)
        gn_t = keep.tile([P, 4], F32, name="gn_t")
        nc.gpsimd.dma_start(gn_t[:], gn.rearrange("(p t) o -> p (t o)", t=4))
        neg_gn = keep.tile([P, 4], F32, name="neg_gn")
        nc.scalar.activation(neg_gn[:], gn_t[:], ACT.Copy, scale=-1.0)
        for a, scales in enumerate((w1_scales, w2_scales)):
            for q in range(4):
                nc.gpsimd.dma_start(
                    ws_raw[32 * q : 32 * q + 4, a * S : (a + 1) * S].bitcast(I32), scales[0, 4 * q : 4 * q + 4, :].bitcast(I32)
                )
        sl_t = keep.tile([P, 4, 8], F32, name="sl_t")
        th_t = keep.tile([P, 4, 8], F32, name="th_t")
        with nc.allow_non_contiguous_dma(reason="one value a row"):
            for tile, src in ((sl_t, sl), (th_t, th)):
                for t in range(4):
                    nc.gpsimd.dma_start(tile[:, t, 0:1], src.rearrange("(a t q) o -> t a q o", t=4, q=4)[t])
        sl_th = keep.tile([P, 4], F32, name="sl_th")
        nc.gpsimd.tensor_tensor(sl_th[:], sl_t[:, :, 0], th_t[:, :, 0], ALU.mult)
        sg_bias = keep.tile([P, 4], F32, name="sg_bias")
        nc.gpsimd.tensor_scalar(sg_bias[:], sl_th[:], -1.0, 0.0, ALU.mult, ALU.add)

        ds_picked = keep.tile([P, 2, S], U8, name="ds_picked")
        xs_picked = keep.tile([P, 2, S], U8, name="xs_picked")
        ds_dealt = keep.tile([P, 2, 4, P], U8, name="ds_dealt")
        nc.vector.tensor_copy(xs_picked[:, 0, :], xs_win[:].indirect(offs_t[:]))
        for a, lst in enumerate((k1_t, k2_t)):
            nc.vector.tensor_copy(ds_picked[:, a, :], ds_win[:].indirect(lst[:]))
        nc.vector.tensor_copy(xs_picked[:, 1, :], xs_win[:].indirect(hz_t[:]))
        place_scale_rows(x_s, xs_picked[:].rearrange("p a c -> p (a c)"))
        nc.vector.tensor_copy(ds_dealt[:].rearrange("p a t m -> p a m t"), ds_picked[:].rearrange("p a (m t) -> p a m t", t=4))
        place_scale_rows(d_s, ds_dealt[:].rearrange("p a t m -> p (a t m)"))

        d_w, x_w = [], []
        for a, (d_lst, x_lst) in enumerate(((k1_t, offs_t), (k2_t, hz_t))):
            picked = placed("dw_picked%d" % a, [P, S], U32, AT_D_PICKED + 2 * ROW * a)
            nc.vector.tensor_copy(picked[:], dw_win[:].indirect(d_lst[:]))
            xw = keep.tile([P, S], U32, name="x_w%d" % a, align_bytes=64)
            nc.vector.tensor_copy(xw[:], xw_win[:].indirect(x_lst[:]))
            x_w.append(xw)
            dealt = keep.tile([P, 4, P], U32, name="d_w%d" % a, align_bytes=64)
            nc.vector.tensor_copy(dealt[:].rearrange("p t m -> p m t"), picked[:].rearrange("p (m t) -> p m t", t=4))
            d_w.append(dealt)

        h_bank = [psum.tile([P, S], F32, name="h_bank%d" % t, tag="bank") for t in range(4)]
        passes = [(t, a) for a in range(2) for t in (0, 1)] + [(t, a) for t in (2, 3) for a in range(2)]
        for t, a in passes:
            nc.tensor.matmul_mx(
                h_bank[t][:], lhsT=d_w[a][:, t, :].bitcast(FP8X4), lhsT_scale=d_s[:, a * S + t * P : a * S + (t + 1) * P],
                rhs=x_w[a][:].bitcast(FP8X4), rhs_scale=x_s[:, a * S : (a + 1) * S],
                start=(a == 0), stop=(a == 1),
            )

        two_picked = placed("two_picked", [P, S], U8, AT_D_PICKED + 2 * ROW + 64 - S)
        two_w = placed("two_w", [P, S], U32, AT_D_PICKED + 2 * ROW + 64)
        nc.vector.tensor_copy(two_picked[:], xs_win[:].indirect(two_t[:]))
        place_scale_rows(two_s, two_picked)
        nc.vector.tensor_copy(two_w[:], xw_win[:].indirect(two_t[:]))
        w_w = []
        for a in range(2):
            dealt = keep.tile([P, 4, 2 * P], U8, name="w_w%d" % a, align_bytes=64)
            nc.scalar.copy(
                dealt[:].bitcast(U32).rearrange("p t (a e) -> p t a e", e=2),
                w_raw[a][:].bitcast(U32).rearrange("p (a t e) -> p t a e", t=4, e=2),
            )
            w_w.append(dealt)

        ub = [keep.tile([P, S], F32, name="ub%d" % t) for t in range(4)]
        pa = [placed("pa%d" % g, [P, 2, W], F32, AT_PAIRS + 2 * ROW * g) for g in range(2)]
        pb = [placed("pb%d" % g, [P, 2, W], F32, AT_PAIRS + 2 * ROW * g + ROW) for g in range(2)]
        rb = [keep.tile([P, 2, W], F32, name="rb%d" % g) for g in range(2)]
        h = [placed("h%d" % t, [P, S], F32, AT_H + ROW * t) for t in range(4)]
        for g in range(2):
            for t in (2 * g, 2 * g + 1):
                nc.scalar.activation(h[t][:], h_bank[t][:], ACT.Copy, scale=0.0625)
            for t in (2 * g, 2 * g + 1):
                piece = LEAD if t == 0 else W
                for first in range(0, W, piece):
                    cols = slice(first, first + piece)
                    nc.scalar.activation(pa[g][:, t % 2, cols], h[t][:].indirect(entries(n1_t, first, piece)), ACT.Copy)
                    nc.scalar.activation(pb[g][:, t % 2, cols], h[t][:].indirect(entries(n2_t, first, piece)), ACT.Copy)
        w_s = placed("w_s", [P, 2, 4, P], U8, AT_H + ROW)
        nc.scalar.copy(w_s[:].bitcast(U32), ws_raw[:].bitcast(U32).rearrange("p (b a t) -> p b t a", b=2, t=4))

        def put_sum(t, first, count):
            cols = slice(first, first + count)
            nc.vector.tensor_tensor(
                ub[t][:].indirect(entries(n3_t, first, count)), pa[t // 2][:, t % 2, cols], pb[t // 2][:, t % 2, cols], ALU.add
            )

        for g in range(2):
            piece = LEAD if g == 0 else W
            for first in range(0, W, piece):
                put_sum(2 * g, first, piece)
            nc.vector.tensor_tensor(rb[g][:], pa[g][:], pb[g][:], ALU.max)
            put_sum(2 * g + 1, 0, W)
            for i in range(2):
                nc.vector.tensor_copy(ub[2 * g + i][:].indirect(n4_t[:]), rb[g][:, i, :])

        z_tiles = placed("z_tiles", [P, 4, S], BF16, AT_PAIRS + 2 * ROW)
        at_scaled = AT_H + 2 * ROW + ROW // 2
        scaled = [placed("scaled%d" % t, [P, S], F32, at_scaled + ROW * t) for t in range(2)]
        scaled.extend(keep.tile([P, S], F32, name="scaled%d" % t) for t in (2, 3))
        far = [placed("far%d" % t, [P, S], F32, at) for t, at in enumerate((AT_FAR, AT_FAR + ROW, at_scaled, AT_FAR))]
        for t in range(2):
            nc.scalar.activation(scaled[t][:], ub[t][:], ACT.Copy, scale=gn_t[:, t : t + 1])
            for first in (0, W):
                nc.scalar.activation(far[t][:, first : first + W], scaled[t][:].indirect(entries(n5_t, first, W)), ACT.Copy)
            nc.gpsimd.tensor_tensor(z_tiles[:, t, :], scaled[t][:], far[t][:], ALU.subtract)
        for t in (2, 3):
            for first in (0, W):
                nc.scalar.activation(far[t][:, first : first + W], ub[t][:].indirect(entries(n5_t, first, W)), ACT.Copy)
        for t in (2, 3):
            nc.vector.tensor_scalar(scaled[t][:], ub[t][:], gn_t[:, t : t + 1], None, ALU.mult)
        for t, cols in ((2, slice(0, S)), (3, slice(0, W)), (3, slice(W, S))):
            nc.vector.scalar_tensor_tensor(
                z_tiles[:, t, cols], far[t][:, cols], neg_gn[:, t : t + 1], scaled[t][:, cols], ALU.mult, ALU.add
            )

        grouped = [keep.tile([P, W, 4], BF16, name="grouped%d" % half, align_bytes=64) for half in range(2)]
        for half, copy in enumerate((nc.vector.tensor_copy, nc.scalar.copy)):
            copy(
                grouped[half][:].rearrange("p (c i) t -> p c t i", i=4),
                z_tiles[:, :, half * W : (half + 1) * W].rearrange("p t (c i) -> p c t i", i=4),
            )
        z_w = keep.tile([P, S], U32, name="z_w", align_bytes=64)
        z_s = keep.tile([P, S], U8, name="z_s", align_bytes=64)
        for half in range(2):
            cols = slice(half * W, (half + 1) * W)
            nc.vector.quantize_mx(z_w[:, cols].bitcast(FP8X4), z_s[:, cols], grouped[half][:].rearrange("p c t -> p (c t)"))

        spans = [(0, slice(0, W)), (0, slice(W, S)), (1, slice(0, S)), (2, slice(0, S)), (3, slice(0, S))]
        h2_bank = [psum.tile([P, cols.stop - cols.start], F32, name="h2_bank%d" % b, tag="bank") for b, (t, cols) in enumerate(spans)]
        for a, (words, scales) in ((1, (two_w, two_s)), (0, (z_w, z_s))):
            for b, (t, cols) in enumerate(spans):
                nc.tensor.matmul_mx(
                    h2_bank[b][:], lhsT=w_w[a][:, t, :].bitcast(FP4X4), lhsT_scale=w_s[:, a, t, :],
                    rhs=words[:, cols].bitcast(FP8X4), rhs_scale=scales[:, cols],
                    start=(a == 1), stop=(a == 0),
                )

        out_rows = out.rearrange("(a t q) j -> t a q j", t=4, q=4)
        ub2 = [keep.tile([P, S], F32, name="ub2_%d" % t) for t in range(4)]
        pa2 = [placed("pa2_%d" % g, [P, 2, W], F32, AT_PAIRS2 + 2 * ROW * g) for g in range(2)]
        pb2 = [placed("pb2_%d" % g, [P, 2, W], F32, AT_PAIRS2 + 2 * ROW * g + ROW) for g in range(2)]
        ra2 = [keep.tile([P, 2, W], F32, name="ra2_%d" % g) for g in range(2)]
        rb2 = [keep.tile([P, 2, W], F32, name="rb2_%d" % g) for g in range(2)]
        h2 = [placed("h2_%d" % t, [P, S], F32, AT_H2 + ROW * t) for t in range(4)]
        for b in (1, 2):
            t, cols = spans[b]
            nc.vector.tensor_copy(h2[t][:, cols], h2_bank[b][:])
        for g, banks in enumerate(((0,), (3, 4))):
            for b in banks:
                t, cols = spans[b]
                nc.scalar.activation(h2[t][:, cols], h2_bank[b][:], ACT.Copy)
            for t in (2 * g, 2 * g + 1):
                piece = LEAD if t == 0 else W
                for first in range(0, W, piece):
                    cols = slice(first, first + piece)
                    nc.scalar.activation(pa2[g][:, t % 2, cols], h2[t][:].indirect(entries(n6_t, first, piece)), ACT.Copy)
                    nc.scalar.activation(pb2[g][:, t % 2, cols], h2[t][:].indirect(entries(n7_t, first, piece)), ACT.Copy)
        flat_a, flat_b, flat_min = (x[:].rearrange("p i c -> p (i c)") for x in (pa2[0], pb2[0], rb2[0]))
        nc.vector.tensor_tensor(ra2[0][:, 0, 0:LEAD], pa2[0][:, 0, 0:LEAD], pb2[0][:, 0, 0:LEAD], ALU.max)
        nc.vector.tensor_tensor(flat_min[:, 0:LEAD], flat_a[:, 0:LEAD], flat_b[:, 0:LEAD], ALU.min)
        nc.vector.tensor_copy(ub2[0][:].indirect(entries(n8_t, 0, LEAD)), ra2[0][:, 0, 0:LEAD])
        nc.vector.tensor_tensor(ra2[0][:, 0, LEAD:W], pa2[0][:, 0, LEAD:W], pb2[0][:, 0, LEAD:W], ALU.max)
        nc.vector.tensor_copy(ub2[0][:].indirect(entries(n8_t, LEAD, W - LEAD)), ra2[0][:, 0, LEAD:W])
        nc.vector.tensor_tensor(ra2[0][:, 1, :], pa2[0][:, 1, :], pb2[0][:, 1, :], ALU.max)
        nc.vector.tensor_tensor(flat_min[:, LEAD:], flat_a[:, LEAD:], flat_b[:, LEAD:], ALU.min)
        nc.vector.tensor_copy(ub2[1][:].indirect(n8_t[:]), ra2[0][:, 1, :])
        for i in range(2):
            nc.vector.tensor_copy(ub2[i][:].indirect(n9_t[:]), rb2[0][:, i, :])
        nc.vector.tensor_tensor(ra2[1][:], pa2[1][:], pb2[1][:], ALU.max)
        nc.vector.tensor_tensor(rb2[1][:], pa2[1][:], pb2[1][:], ALU.min)
        for lst, values in ((n8_t, ra2[1]), (n9_t, rb2[1])):
            for i in range(2):
                nc.vector.tensor_copy(ub2[2 + i][:].indirect(lst[:]), values[:, i, :])

        for t in range(4):
            sg = placed("sg%d" % t, [P, S], F32, AT_H2 + 2 * ROW + ROW // 2 + ROW * t)
            if t < 2:
                res = placed("res%d" % t, [P, S], F32, AT_PAIRS2 + 2 * ROW + ROW * t)
            else:
                res = keep.tile([P, S], F32, name="res%d" % t)
            pieces = [(0, W), (W, W)] if t < 3 else [(0, W), (W, LEAD), (W + LEAD, LEAD)]
            for first, count in pieces:
                nc.scalar.activation(
                    sg[:, first : first + count], ub2[t][:].indirect(entries(n10_t, first, count)), ACT.Sigmoid,
                    scale=sl_t[:, t, 0:1], bias=sg_bias[:, t : t + 1],
                )
            engine = nc.gpsimd if t < 2 else nc.vector
            for first, count in ([(0, S)] if t < 3 else pieces):
                cols = slice(first, first + count)
                engine.tensor_tensor(res[:, cols], ub2[t][:, cols], sg[:, cols], ALU.mult)
                nc.sync.dma_start(out_rows[t][:, :, cols], res[:, cols])
